import numpy as np
import ml_dtypes


def mxq(x, axis, fmt="e4m3"):
    dtype, down = {"e4m3": (ml_dtypes.float8_e4m3fn, 7), "e5m2": (ml_dtypes.float8_e5m2, 14)}[fmt]
    v = np.moveaxis(np.asarray(x, np.float32).astype(ml_dtypes.bfloat16).astype(np.float64), axis, -1)
    blocks = v.reshape(v.shape[:-1] + (-1, 32))
    amax = np.abs(blocks).max(-1, keepdims=True)
    byte = np.maximum(np.where(amax > 0, np.frexp(amax)[1] - 1 + 127, 0) - down, 1)
    scale = np.exp2(byte - 127.0)
    codes = (blocks / scale).astype(np.float32).astype(dtype).astype(np.float64)
    return np.moveaxis((codes * scale).reshape(v.shape), -1, axis)


WIDE = False


def mx_kscale(k):
    if not WIDE:
        return np.ones(k)
    levels = np.array([10, -10, 5, -5, 0])
    if k % 512:
        return np.exp2(np.random.permutation(np.resize(levels, k // 32))).repeat(32)
    a = np.empty((k // 512, 16))
    for p in range(k // 512):
        a[p, :8] = np.random.permutation(np.resize(levels, 8))
        for g in range(8):
            far = levels[np.abs(levels - a[p, g]) >= 10]
            a[p, g + 8] = far[np.random.randint(len(far))]
    return np.exp2(a.ravel()).repeat(32)


def f64(x):
    return np.asarray(x).astype(np.float64)


def striped(idx):
    return np.tile(np.asarray(idx).reshape(-1, 16).T, (8, 1)).astype(np.uint16)


def unstriped(offs):
    return offs[:16].T.reshape(-1).astype(np.int64)


B, N, T, D, DV, NQ = 1, 512, 2048, 256, 512, 1024


def setup_inputs():
    n = np.random.standard_normal
    idx = np.random.permutation(T)[:B * N]
    s = mx_kscale(DV)[:, None]
    z = mx_kscale(NQ)[:, None]
    p = np.exp(n((B, NQ, N)))
    p = p / p.mean(2, keepdims=True)
    return {
        "doT": (n((B, DV, NQ)) * s / np.sqrt(DV)).astype(np.float32),
        "vT": (n((DV, T)) / s).astype(np.float32),
        "p": (p * z / np.sqrt(NQ)).astype(np.float32),
        "delta": (0.3 * n((B, NQ, 1))).astype(np.float32),
        "qm": (n((B, NQ, D)) / z).astype(np.float32),
        "offs": striped(idx),
    }


def reference(doT, vT, p, delta, qm, offs):
    idx = unstriped(offs)
    pick = lambda x: x[:, idx].reshape(x.shape[0], B, N).transpose(1, 0, 2)
    dp = mxq(f64(doT), 1, "e4m3").transpose(0, 2, 1) @ mxq(pick(f64(vT)), 1, "e4m3")
    ds = f64(p) * (dp - f64(delta))
    dk = mxq(f64(qm), 1, "e4m3").transpose(0, 2, 1) @ mxq(ds, 1, "e4m3")
    out = np.zeros((D, T))
    out[:, idx] = dk.transpose(1, 0, 2).reshape(D, B * N)
    return out

@@ -1,0 +1,167 @@
+from contextlib import ExitStack
+
+import concourse.mybir as mybir
+
+DV, NQ, N, T, D = 512, 1024, 512, 2048, 256
+FLOPS = 2 * NQ * N * DV + 2 * D * N * NQ
+
+F32 = mybir.dt.float32
+BF16 = mybir.dt.bfloat16
+U32 = mybir.dt.uint32
+U16 = mybir.dt.uint16
+U8 = mybir.dt.uint8
+FP8X4 = mybir.dt.float8_e4m3fn_x4
+SUB = mybir.AluOpType.subtract
+MULT = mybir.AluOpType.mult
+
+P = 128
+PACK = 4
+KP = P * PACK
+G = NQ // KP
+H = D // P
+P_CUTS = [[(0, 2), (2, 2)], [(0, 2), (2, 1), (3, 1)]]
+
+
+def tile_attend_bwd_kernel(tc, doT, vT, p, delta, qm, offs, out):
+    nc = tc.nc
+    doT2 = doT.flatten_outer_dims()
+    p2 = p.flatten_outer_dims()
+    delta2 = delta.flatten_outer_dims()
+    qm2 = qm.flatten_outer_dims()
+
+    with ExitStack() as ctx:
+        lists = ctx.enter_context(tc.tile_pool(name="lists", bufs=1))
+        keep = ctx.enter_context(tc.tile_pool(name="keep", bufs=1))
+        psum = ctx.enter_context(tc.psum_pool(name="psum", bufs=1))
+
+        offsets = lists.tile([P, N // 16], U16, name="offsets")
+        nc.sync.dma_start(offsets[:], offs)
+
+        do_raw = [keep.tile([P, PACK, KP], F32, name=f"do_raw{g}") for g in range(G)]
+        v_raw = [keep.tile([P, T], F32, name=f"v_raw{t}") for t in range(PACK)]
+        p_raw = [[keep.tile([P, w, N], F32, name=f"p_raw{g}_{t}") for t, w in P_CUTS[g]] for g in range(G)]
+        qm_raw = [keep.tile([P, PACK, D], F32, name=f"qm_raw{g}") for g in range(G)]
+        dlt = keep.tile([P, G, PACK], F32, name="dlt")
+
+        do_rows = doT2.rearrange("(p j) q -> p j q", j=PACK)
+        v_rows = vT.rearrange("(p j) n -> p j n", j=PACK)
+        p_rows = p2.rearrange("(g p t) n -> g p t n", g=G, t=PACK)
+        qm_rows = qm2.rearrange("(g p t) d -> g p t d", g=G, t=PACK)
+
+        nc.scalar.dma_start(dlt[:], delta2.rearrange("(g p t) x -> p g (t x)", g=G, t=PACK))
+        nc.sync.dma_start(do_raw[0][:], do_rows[:, :, 0:KP])
+        for t in range(PACK):
+            nc.sync.dma_start(v_raw[t][:], v_rows[:, t, :])
+        nc.sync.dma_start(do_raw[1][:], do_rows[:, :, KP:2 * KP])
+        for g in range(G):
+            for i, (t, w) in enumerate(P_CUTS[g]):
+                nc.sync.dma_start(p_raw[g][i][:], p_rows[g, :, t:t + w, :])
+        for g in range(G):
+            nc.sync.dma_start(qm_raw[g][:], qm_rows[g])
+
+        window = [keep.tile([P, T], F32, name=f"window{h}") for h in range(H)]
+        for h in range(H):
+            nc.vector.memset(window[h][:], 0.0)
+
+        do_bf = [keep.tile([P, KP, PACK], BF16, name=f"do_bf{g}", align_bytes=64) for g in range(G)]
+        do_codes = [keep.tile([P, KP], U32, name=f"do_codes{g}", align_bytes=64) for g in range(G)]
+        do_scales = [keep.tile([P, KP], U8, name=f"do_scales{g}", align_bytes=64) for g in range(G)]
+        v_bf = keep.tile([P, N, PACK], BF16, name="v_bf", align_bytes=64)
+        v_codes = keep.tile([P, N], U32, name="v_codes", align_bytes=64)
+        v_scales = keep.tile([P, N], U8, name="v_scales", align_bytes=64)
+        ds_pl = [keep.tile([P, PACK, N], BF16, name=f"ds_pl{g}", align_bytes=64) for g in range(G)]
+        ds_bf = [keep.tile([P, N, PACK], BF16, name=f"ds_bf{g}", align_bytes=64) for g in range(G)]
+        ds_codes = [keep.tile([P, N], U32, name=f"ds_codes{g}", align_bytes=64) for g in range(G)]
+        ds_scales = [keep.tile([P, N], U8, name=f"ds_scales{g}", align_bytes=64) for g in range(G)]
+        qm_bf = [keep.tile([P, D, PACK], BF16, name=f"qm_bf{g}", align_bytes=64) for g in range(G)]
+        qm_codes = [keep.tile([P, D], U32, name=f"qm_codes{g}", align_bytes=64) for g in range(G)]
+        qm_scales = [keep.tile([P, D], U8, name=f"qm_scales{g}", align_bytes=64) for g in range(G)]
+        res = [keep.tile([P, N], F32, name=f"res{h}") for h in range(H)]
+
+        dp = [psum.tile([P, N], F32, name=f"dp{i}") for i in range(6)]
+        dk = [psum.tile([P, N], F32, name=f"dk{h}") for h in range(H)]
+
+        def quant(codes, scales, src):
+            nc.vector.quantize_mx(out=codes.bitcast(FP8X4), scales=scales, in_=src.rearrange("p w j -> p (w j)"))
+
+        def interleave_do(g):
+            nc.scalar.copy(
+                out=do_bf[g][:].rearrange("p (t m) j -> p m j t", t=PACK),
+                in_=do_raw[g][:].rearrange("p j (m t) -> p m j t", t=PACK),
+            )
+
+        interleave_do(0)
+        for t in range(PACK):
+            nc.vector.tensor_copy(v_bf[:, :, t], v_raw[t][:].indirect(offsets[:]))
+        quant(do_codes[0][:], do_scales[0][:], do_bf[0][:])
+        quant(v_codes[:], v_scales[:], v_bf[:])
+        interleave_do(1)
+
+        def product_dp(g, t):
+            bank = dp[(g * PACK + t) % 6]
+            cols = slice(t * P, (t + 1) * P)
+            nc.tensor.matmul_mx(
+                out=bank[:],
+                lhsT=do_codes[g][:, cols].bitcast(FP8X4), lhsT_scale=do_scales[g][:, cols],
+                rhs=v_codes[:].bitcast(FP8X4), rhs_scale=v_scales[:],
+                start=True, stop=True,
+            )
+            return bank
+
+        def p_plane(g, t):
+            for i, (t0, w) in enumerate(P_CUTS[g]):
+                if t0 <= t < t0 + w:
+                    return p_raw[g][i][:, t - t0, :]
+
+        def weigh(g, t):
+            bank = product_dp(g, t)
+            nc.vector.scalar_tensor_tensor(ds_pl[g][:, t, :], bank[:], dlt[:, g, t:t + 1], p_plane(g, t), SUB, MULT)
+
+        def interleave_ds(copy, g, t0, t1):
+            copy(
+                out=ds_bf[g][:, :, t0:t1].rearrange("p (c i) t -> p c t i", i=8),
+                in_=ds_pl[g][:, t0:t1, :].rearrange("p t (c i) -> p c t i", i=8),
+            )
+
+        def interleave_qm(copy, g, cols):
+            copy(
+                out=qm_bf[g][:, cols, :].rearrange("p (c i) t -> p c t i", i=4),
+                in_=qm_raw[g][:, :, cols].rearrange("p t (c i) -> p c t i", i=4),
+            )
+
+        weigh(0, 0)
+        weigh(0, 1)
+        weigh(0, 2)
+        quant(do_codes[1][:], do_scales[1][:], do_bf[1][:])
+        weigh(0, 3)
+        interleave_ds(nc.scalar.copy, 0, 0, 4)
+        weigh(1, 0)
+        weigh(1, 1)
+        interleave_ds(nc.scalar.copy, 1, 0, 2)
+        weigh(1, 2)
+        quant(ds_codes[0][:], ds_scales[0][:], ds_bf[0][:])
+        weigh(1, 3)
+        interleave_ds(nc.vector.tensor_copy, 1, 2, 4)
+        interleave_qm(nc.scalar.copy, 0, slice(0, D))
+        quant(ds_codes[1][:], ds_scales[1][:], ds_bf[1][:])
+        quant(qm_codes[0][:], qm_scales[0][:], qm_bf[0][:])
+        halves = [slice(h * P, (h + 1) * P) for h in range(H)]
+        interleave_qm(nc.vector.tensor_copy, 1, halves[0])
+        interleave_qm(nc.scalar.copy, 1, halves[1])
+
+        for h in range(H):
+            cols = halves[h]
+            quant(qm_codes[1][:, cols], qm_scales[1][:, cols], qm_bf[1][:, cols, :])
+            for g in range(G):
+                nc.tensor.matmul_mx(
+                    out=dk[h][:],
+                    lhsT=qm_codes[g][:, cols].bitcast(FP8X4), lhsT_scale=qm_scales[g][:, cols],
+                    rhs=ds_codes[g][:].bitcast(FP8X4), rhs_scale=ds_scales[g][:],
+                    start=(g == 0), stop=(g == G - 1),
+                )
+            nc.scalar.copy(out=res[h][:], in_=dk[h][:])
+        for h in range(H):
+            nc.vector.tensor_copy(window[h][:].indirect(offsets[:]), res[h][:])
+            for k in range(2):
+                span = slice(k * T // 2, (k + 1) * T // 2)
+                (nc.sync if k == 0 else nc.scalar).dma_start(out[h * P:(h + 1) * P, span], window[h][:, span])

@@ -19,7 +19,8 @@ PACK = 4
 KP = P * PACK
 G = NQ // KP
 H = D // P
-P_CUTS = [[(0, 2), (2, 2)], [(0, 2), (2, 1), (3, 1)]]
+NH = N // 2
+P_CUTS = [(0, 2), (2, 2)]
 
 
 def tile_attend_bwd_kernel(tc, doT, vT, p, delta, qm, offs, out):
@@ -39,7 +40,7 @@ def tile_attend_bwd_kernel(tc, doT, vT, p, delta, qm, offs, out):
 
         do_raw = [keep.tile([P, PACK, KP], F32, name=f"do_raw{g}") for g in range(G)]
         v_raw = [keep.tile([P, T], F32, name=f"v_raw{t}") for t in range(PACK)]
-        p_raw = [[keep.tile([P, w, N], F32, name=f"p_raw{g}_{t}") for t, w in P_CUTS[g]] for g in range(G)]
+        p_raw = [[keep.tile([P, w, N], F32, name=f"p_raw{g}_{t}") for t, w in P_CUTS] for g in range(G)]
         qm_raw = [keep.tile([P, PACK, D], F32, name=f"qm_raw{g}") for g in range(G)]
         dlt = keep.tile([P, G, PACK], F32, name="dlt")
 
@@ -49,15 +50,21 @@ def tile_attend_bwd_kernel(tc, doT, vT, p, delta, qm, offs, out):
         qm_rows = qm2.rearrange("(g p t) d -> g p t d", g=G, t=PACK)
 
         nc.scalar.dma_start(dlt[:], delta2.rearrange("(g p t) x -> p g (t x)", g=G, t=PACK))
-        nc.sync.dma_start(do_raw[0][:], do_rows[:, :, 0:KP])
+        def load_do(g):
+            nc.sync.dma_start(do_raw[g][:], do_rows[:, :, g * KP:(g + 1) * KP])
+
+        def load_p(g):
+            for i, (t, w) in enumerate(P_CUTS):
+                nc.sync.dma_start(p_raw[g][i][:], p_rows[g, :, t:t + w, :])
+
+        load_do(0)
         for t in range(PACK):
             nc.sync.dma_start(v_raw[t][:], v_rows[:, t, :])
-        nc.sync.dma_start(do_raw[1][:], do_rows[:, :, KP:2 * KP])
-        for g in range(G):
-            for i, (t, w) in enumerate(P_CUTS[g]):
-                nc.sync.dma_start(p_raw[g][i][:], p_rows[g, :, t:t + w, :])
-        for g in range(G):
-            nc.sync.dma_start(qm_raw[g][:], qm_rows[g])
+        load_do(1)
+        load_p(0)
+        nc.sync.dma_start(qm_raw[1][:], qm_rows[1])
+        load_p(1)
+        nc.sync.dma_start(qm_raw[0][:], qm_rows[0])
 
         window = [keep.tile([P, T], F32, name=f"window{h}") for h in range(H)]
         for h in range(H):
@@ -78,27 +85,28 @@ def tile_attend_bwd_kernel(tc, doT, vT, p, delta, qm, offs, out):
         qm_scales = [keep.tile([P, D], U8, name=f"qm_scales{g}", align_bytes=64) for g in range(G)]
         res = [keep.tile([P, N], F32, name=f"res{h}") for h in range(H)]
 
-        dp = [psum.tile([P, N], F32, name=f"dp{i}") for i in range(6)]
-        dk = [psum.tile([P, N], F32, name=f"dk{h}") for h in range(H)]
+        dp = [[psum.tile([P, N], F32, name=f"dp{g}_{t}", tag=f"bank{g * PACK + t}") for t in range(PACK)] for g in range(G)]
 
         def quant(codes, scales, src):
             nc.vector.quantize_mx(out=codes.bitcast(FP8X4), scales=scales, in_=src.rearrange("p w j -> p (w j)"))
 
-        def interleave_do(g):
-            nc.scalar.copy(
-                out=do_bf[g][:].rearrange("p (t m) j -> p m j t", t=PACK),
-                in_=do_raw[g][:].rearrange("p j (m t) -> p m j t", t=PACK),
+        def interleave_do(copy, g, m0, m1):
+            copy(
+                out=do_bf[g][:].rearrange("p (t m) j -> p m j t", t=PACK)[:, m0:m1],
+                in_=do_raw[g][:].rearrange("p j (m t) -> p m j t", t=PACK)[:, m0:m1],
             )
 
-        interleave_do(0)
+        interleave_do(nc.scalar.copy, 0, 0, P)
         for t in range(PACK):
             nc.vector.tensor_copy(v_bf[:, :, t], v_raw[t][:].indirect(offsets[:]))
         quant(do_codes[0][:], do_scales[0][:], do_bf[0][:])
         quant(v_codes[:], v_scales[:], v_bf[:])
-        interleave_do(1)
+        interleave_do(nc.vector.tensor_copy, 1, 0, P // 2)
+        interleave_do(nc.scalar.copy, 1, P // 2, P)
+        quant(do_codes[1][:], do_scales[1][:], do_bf[1][:])
 
         def product_dp(g, t):
-            bank = dp[(g * PACK + t) % 6]
+            bank = dp[g][t]
             cols = slice(t * P, (t + 1) * P)
             nc.tensor.matmul_mx(
                 out=bank[:],
@@ -109,7 +117,7 @@ def tile_attend_bwd_kernel(tc, doT, vT, p, delta, qm, offs, out):
             return bank
 
         def p_plane(g, t):
-            for i, (t0, w) in enumerate(P_CUTS[g]):
+            for i, (t0, w) in enumerate(P_CUTS):
                 if t0 <= t < t0 + w:
                     return p_raw[g][i][:, t - t0, :]
 
@@ -117,10 +125,10 @@ def tile_attend_bwd_kernel(tc, doT, vT, p, delta, qm, offs, out):
             bank = product_dp(g, t)
             nc.vector.scalar_tensor_tensor(ds_pl[g][:, t, :], bank[:], dlt[:, g, t:t + 1], p_plane(g, t), SUB, MULT)
 
-        def interleave_ds(copy, g, t0, t1):
+        def interleave_ds(copy, g, t0, t1, cols):
             copy(
-                out=ds_bf[g][:, :, t0:t1].rearrange("p (c i) t -> p c t i", i=8),
-                in_=ds_pl[g][:, t0:t1, :].rearrange("p t (c i) -> p c t i", i=8),
+                out=ds_bf[g][:, cols, t0:t1].rearrange("p (c i) t -> p c t i", i=8),
+                in_=ds_pl[g][:, t0:t1, cols].rearrange("p t (c i) -> p c t i", i=8),
             )
 
         def interleave_qm(copy, g, cols):
@@ -129,39 +137,50 @@ def tile_attend_bwd_kernel(tc, doT, vT, p, delta, qm, offs, out):
                 in_=qm_raw[g][:, :, cols].rearrange("p t (c i) -> p c t i", i=4),
             )
 
-        weigh(0, 0)
-        weigh(0, 1)
-        weigh(0, 2)
-        quant(do_codes[1][:], do_scales[1][:], do_bf[1][:])
-        weigh(0, 3)
-        interleave_ds(nc.scalar.copy, 0, 0, 4)
-        weigh(1, 0)
-        weigh(1, 1)
-        interleave_ds(nc.scalar.copy, 1, 0, 2)
-        weigh(1, 2)
-        quant(ds_codes[0][:], ds_scales[0][:], ds_bf[0][:])
-        weigh(1, 3)
-        interleave_ds(nc.vector.tensor_copy, 1, 2, 4)
-        interleave_qm(nc.scalar.copy, 0, slice(0, D))
-        quant(ds_codes[1][:], ds_scales[1][:], ds_bf[1][:])
-        quant(qm_codes[0][:], qm_scales[0][:], qm_bf[0][:])
-        halves = [slice(h * P, (h + 1) * P) for h in range(H)]
-        interleave_qm(nc.vector.tensor_copy, 1, halves[0])
-        interleave_qm(nc.scalar.copy, 1, halves[1])
+        def quant_qm(g, cols):
+            quant(qm_codes[g][:, cols], qm_scales[g][:, cols], qm_bf[g][:, cols, :])
 
+        def quant_ds(g, cols):
+            quant(ds_codes[g][:, cols], ds_scales[g][:, cols], ds_bf[g][:, cols, :])
+
+        def product_dk(h, s, g):
+            d = slice(h * P, (h + 1) * P)
+            n = slots[s]
+            nc.tensor.matmul_mx(
+                out=dk[h][s][:],
+                lhsT=qm_codes[g][:, d].bitcast(FP8X4), lhsT_scale=qm_scales[g][:, d],
+                rhs=ds_codes[g][:, n].bitcast(FP8X4), rhs_scale=ds_scales[g][:, n],
+                start=(g == 0), stop=(g == G - 1),
+            )
+
+        every = slice(0, N)
+        slots = [slice(s * NH, (s + 1) * NH) for s in range(2)]
+        halves = [slice(h * P, (h + 1) * P) for h in range(H)]
+        for t in range(PACK):
+            weigh(0, t)
+        interleave_qm(nc.scalar.copy, 1, slice(0, D))
+        quant_qm(1, slice(0, D))
+        interleave_ds(nc.scalar.copy, 0, 0, 4, every)
+        for t in range(PACK):
+            weigh(1, t)
+        interleave_qm(nc.vector.tensor_copy, 0, halves[0])
+        interleave_qm(nc.scalar.copy, 0, halves[1])
+        interleave_ds(nc.vector.tensor_copy, 1, 0, 4, slice(0, P))
+        interleave_ds(nc.scalar.copy, 1, 0, 4, slice(P, 2 * P))
+        interleave_ds(nc.scalar.copy, 1, 0, 4, slots[1])
+        quant_ds(0, every)
+        quant_ds(1, slots[0])
+        quant_qm(0, slice(0, D))
+        quant_ds(1, slots[1])
+        dk = [[psum.tile([P, NH], F32, name=f"dk{h}_{s}", tag=f"bank{2 * h + s}") for s in range(2)] for h in range(H)]
         for h in range(H):
-            cols = halves[h]
-            quant(qm_codes[1][:, cols], qm_scales[1][:, cols], qm_bf[1][:, cols, :])
-            for g in range(G):
-                nc.tensor.matmul_mx(
-                    out=dk[h][:],
-                    lhsT=qm_codes[g][:, cols].bitcast(FP8X4), lhsT_scale=qm_scales[g][:, cols],
-                    rhs=ds_codes[g][:].bitcast(FP8X4), rhs_scale=ds_scales[g][:],
-                    start=(g == 0), stop=(g == G - 1),
-                )
-            nc.scalar.copy(out=res[h][:], in_=dk[h][:])
+            for s in range(2):
+                for g in range(G):
+                    product_dk(h, s, g)
+                nc.scalar.copy(out=res[h][:, slots[s]], in_=dk[h][s][:])
         for h in range(H):
-            nc.vector.tensor_copy(window[h][:].indirect(offsets[:]), res[h][:])
+            for s in range(2):
+                nc.vector.tensor_copy(window[h][:].indirect(offsets[:, s * NH // 16:(s + 1) * NH // 16]), res[h][:, slots[s]])
             for k in range(2):
                 span = slice(k * T // 2, (k + 1) * T // 2)
                 (nc.sync if k == 0 else nc.scalar).dma_start(out[h * P:(h + 1) * P, span], window[h][:, span])

@@ -11,6 +11,8 @@ U32 = mybir.dt.uint32
 U16 = mybir.dt.uint16
 U8 = mybir.dt.uint8
 FP8X4 = mybir.dt.float8_e4m3fn_x4
+IDENTITY = mybir.ActivationFunctionType.Identity
+ADD = mybir.AluOpType.add
 SUB = mybir.AluOpType.subtract
 MULT = mybir.AluOpType.mult
 
@@ -36,35 +38,39 @@ def tile_attend_bwd_kernel(tc, doT, vT, p, delta, qm, offs, out):
         psum = ctx.enter_context(tc.psum_pool(name="psum", bufs=1))
 
         offsets = lists.tile([P, N // 16], U16, name="offsets")
-        nc.sync.dma_start(offsets[:], offs)
 
         do_raw = [keep.tile([P, PACK, KP], F32, name=f"do_raw{g}") for g in range(G)]
         v_raw = [keep.tile([P, T], F32, name=f"v_raw{t}") for t in range(PACK)]
         p_raw = [[keep.tile([P, w, N], F32, name=f"p_raw{g}_{t}") for t, w in P_CUTS] for g in range(G)]
         qm_raw = [keep.tile([P, PACK, D], F32, name=f"qm_raw{g}") for g in range(G)]
         dlt = keep.tile([P, G, PACK], F32, name="dlt")
+        ndlt = keep.tile([P, G, PACK], F32, name="ndlt")
+        x = [keep.tile([P, N], F32, name=f"x{g}") for g in range(G)]
 
         do_rows = doT2.rearrange("(p j) q -> p j q", j=PACK)
         v_rows = vT.rearrange("(p j) n -> p j n", j=PACK)
         p_rows = p2.rearrange("(g p t) n -> g p t n", g=G, t=PACK)
         qm_rows = qm2.rearrange("(g p t) d -> g p t d", g=G, t=PACK)
 
-        nc.scalar.dma_start(dlt[:], delta2.rearrange("(g p t) x -> p g (t x)", g=G, t=PACK))
         def load_do(g):
             nc.sync.dma_start(do_raw[g][:], do_rows[:, :, g * KP:(g + 1) * KP])
 
-        def load_p(g):
-            for i, (t, w) in enumerate(P_CUTS):
-                nc.sync.dma_start(p_raw[g][i][:], p_rows[g, :, t:t + w, :])
+        def load_p(g, i):
+            t, w = P_CUTS[i]
+            nc.sync.dma_start(p_raw[g][i][:], p_rows[g, :, t:t + w, :])
 
         load_do(0)
+        nc.sync.dma_start(offsets[:], offs)
         for t in range(PACK):
             nc.sync.dma_start(v_raw[t][:], v_rows[:, t, :])
         load_do(1)
-        load_p(0)
-        nc.sync.dma_start(qm_raw[1][:], qm_rows[1])
-        load_p(1)
-        nc.sync.dma_start(qm_raw[0][:], qm_rows[0])
+        nc.sync.dma_start(dlt[:], delta2.rearrange("(g p t) x -> p g (t x)", g=G, t=PACK))
+        load_p(0, 0)
+        load_p(0, 1)
+        load_p(1, 0)
+        load_p(1, 1)
+        for g in range(G):
+            nc.sync.dma_start(qm_raw[g][:], qm_rows[g])
 
         window = [keep.tile([P, T], F32, name=f"window{h}") for h in range(H)]
         for h in range(H):
@@ -123,6 +129,10 @@ def tile_attend_bwd_kernel(tc, doT, vT, p, delta, qm, offs, out):
 
         def weigh(g, t):
             bank = product_dp(g, t)
+            if t == g:
+                nc.scalar.activation(x[g][:], bank[:], IDENTITY, bias=ndlt[:, g, t:t + 1], scale=1.0)
+                nc.gpsimd.tensor_tensor(ds_pl[g][:, t, :], x[g][:], p_plane(g, t), MULT)
+                return
             nc.vector.scalar_tensor_tensor(ds_pl[g][:, t, :], bank[:], dlt[:, g, t:t + 1], p_plane(g, t), SUB, MULT)
 
         def interleave_ds(copy, g, t0, t1, cols):
@@ -143,11 +153,10 @@ def tile_attend_bwd_kernel(tc, doT, vT, p, delta, qm, offs, out):
         def quant_ds(g, cols):
             quant(ds_codes[g][:, cols], ds_scales[g][:, cols], ds_bf[g][:, cols, :])
 
-        def product_dk(h, s, g):
+        def product_dk(bank, h, n, g):
             d = slice(h * P, (h + 1) * P)
-            n = slots[s]
             nc.tensor.matmul_mx(
-                out=dk[h][s][:],
+                out=bank[:],
                 lhsT=qm_codes[g][:, d].bitcast(FP8X4), lhsT_scale=qm_scales[g][:, d],
                 rhs=ds_codes[g][:, n].bitcast(FP8X4), rhs_scale=ds_scales[g][:, n],
                 start=(g == 0), stop=(g == G - 1),
@@ -155,32 +164,33 @@ def tile_attend_bwd_kernel(tc, doT, vT, p, delta, qm, offs, out):
 
         every = slice(0, N)
         slots = [slice(s * NH, (s + 1) * NH) for s in range(2)]
-        halves = [slice(h * P, (h + 1) * P) for h in range(H)]
+
+        nc.gpsimd.tensor_scalar(ndlt[:], dlt[:], -1.0, 0.0, MULT, ADD)
         for t in range(PACK):
             weigh(0, t)
-        interleave_qm(nc.scalar.copy, 1, slice(0, D))
-        quant_qm(1, slice(0, D))
         interleave_ds(nc.scalar.copy, 0, 0, 4, every)
         for t in range(PACK):
             weigh(1, t)
-        interleave_qm(nc.vector.tensor_copy, 0, halves[0])
-        interleave_qm(nc.scalar.copy, 0, halves[1])
-        interleave_ds(nc.vector.tensor_copy, 1, 0, 4, slice(0, P))
-        interleave_ds(nc.scalar.copy, 1, 0, 4, slice(P, 2 * P))
-        interleave_ds(nc.scalar.copy, 1, 0, 4, slots[1])
+        interleave_qm(nc.vector.tensor_copy, 0, slice(0, D))
+        quant_qm(0, slice(0, D))
+        for s in range(2):
+            interleave_ds(nc.scalar.copy, 1, 0, 4, slots[s])
+        interleave_qm(nc.vector.tensor_copy, 1, slice(0, D))
         quant_ds(0, every)
         quant_ds(1, slots[0])
-        quant_qm(0, slice(0, D))
+        quant_qm(1, slice(0, D))
         quant_ds(1, slots[1])
-        dk = [[psum.tile([P, NH], F32, name=f"dk{h}_{s}", tag=f"bank{2 * h + s}") for s in range(2)] for h in range(H)]
+        dk = [[psum.tile([P, NH], F32, name=f"dk0_{s}", tag=f"bank{s}") for s in range(2)],
+              [psum.tile([P, N], F32, name="dk1", tag="bank2")]]
+        cuts = [slots, [every]]
         for h in range(H):
-            for s in range(2):
+            for bank, n in zip(dk[h], cuts[h]):
                 for g in range(G):
-                    product_dk(h, s, g)
-                nc.scalar.copy(out=res[h][:, slots[s]], in_=dk[h][s][:])
+                    product_dk(bank, h, n, g)
+                nc.scalar.copy(out=res[h][:, n], in_=bank[:])
         for h in range(H):
-            for s in range(2):
-                nc.vector.tensor_copy(window[h][:].indirect(offsets[:, s * NH // 16:(s + 1) * NH // 16]), res[h][:, slots[s]])
+            for n in cuts[h]:
+                nc.vector.tensor_copy(window[h][:].indirect(offsets[:, n.start // 16:n.stop // 16]), res[h][:, n])
             for k in range(2):
                 span = slice(k * T // 2, (k + 1) * T // 2)
                 (nc.sync if k == 0 else nc.scalar).dma_start(out[h * P:(h + 1) * P, span], window[h][:, span])

from contextlib import ExitStack

import concourse.mybir as mybir

DV, NQ, N, T, D = 512, 1024, 512, 2048, 256
FLOPS = 2 * NQ * N * DV + 2 * D * N * NQ

F32 = mybir.dt.float32
BF16 = mybir.dt.bfloat16
U32 = mybir.dt.uint32
U16 = mybir.dt.uint16
U8 = mybir.dt.uint8
FP8X4 = mybir.dt.float8_e4m3fn_x4
IDENTITY = mybir.ActivationFunctionType.Identity
ADD = mybir.AluOpType.add
SUB = mybir.AluOpType.subtract
MULT = mybir.AluOpType.mult

P = 128
PACK = 4
KP = P * PACK
G = NQ // KP
H = D // P
NH = N // 2
P_CUTS = [(0, 2), (2, 2)]


def tile_attend_bwd_kernel(tc, doT, vT, p, delta, qm, offs, out):
    nc = tc.nc
    doT2 = doT.flatten_outer_dims()
    p2 = p.flatten_outer_dims()
    delta2 = delta.flatten_outer_dims()
    qm2 = qm.flatten_outer_dims()

    with ExitStack() as ctx:
        lists = ctx.enter_context(tc.tile_pool(name="lists", bufs=1))
        keep = ctx.enter_context(tc.tile_pool(name="keep", bufs=1))
        psum = ctx.enter_context(tc.psum_pool(name="psum", bufs=1))

        offsets = lists.tile([P, N // 16], U16, name="offsets")

        do_raw = [keep.tile([P, PACK, KP], F32, name=f"do_raw{g}") for g in range(G)]
        v_raw = [keep.tile([P, T], F32, name=f"v_raw{t}") for t in range(PACK)]
        p_raw = [[keep.tile([P, w, N], F32, name=f"p_raw{g}_{t}") for t, w in P_CUTS] for g in range(G)]
        qm_raw = [keep.tile([P, PACK, D], F32, name=f"qm_raw{g}") for g in range(G)]
        dlt = keep.tile([P, G, PACK], F32, name="dlt")
        ndlt = keep.tile([P, G, PACK], F32, name="ndlt")
        x = [keep.tile([P, N], F32, name=f"x{g}") for g in range(G)]

        do_rows = doT2.rearrange("(p j) q -> p j q", j=PACK)
        v_rows = vT.rearrange("(p j) n -> p j n", j=PACK)
        p_rows = p2.rearrange("(g p t) n -> g p t n", g=G, t=PACK)
        qm_rows = qm2.rearrange("(g p t) d -> g p t d", g=G, t=PACK)

        def load_do(g):
            nc.sync.dma_start(do_raw[g][:], do_rows[:, :, g * KP:(g + 1) * KP])

        def load_p(g, i):
            t, w = P_CUTS[i]
            nc.sync.dma_start(p_raw[g][i][:], p_rows[g, :, t:t + w, :])

        load_do(0)
        nc.sync.dma_start(offsets[:], offs)
        for t in range(PACK):
            nc.sync.dma_start(v_raw[t][:], v_rows[:, t, :])
        load_do(1)
        nc.sync.dma_start(dlt[:], delta2.rearrange("(g p t) x -> p g (t x)", g=G, t=PACK))
        load_p(0, 0)
        load_p(0, 1)
        load_p(1, 0)
        load_p(1, 1)
        for g in range(G):
            nc.sync.dma_start(qm_raw[g][:], qm_rows[g])

        window = [keep.tile([P, T], F32, name=f"window{h}") for h in range(H)]
        for h in range(H):
            nc.vector.memset(window[h][:], 0.0)

        do_bf = [keep.tile([P, KP, PACK], BF16, name=f"do_bf{g}", align_bytes=64) for g in range(G)]
        do_codes = [keep.tile([P, KP], U32, name=f"do_codes{g}", align_bytes=64) for g in range(G)]
        do_scales = [keep.tile([P, KP], U8, name=f"do_scales{g}", align_bytes=64) for g in range(G)]
        v_bf = keep.tile([P, N, PACK], BF16, name="v_bf", align_bytes=64)
        v_codes = keep.tile([P, N], U32, name="v_codes", align_bytes=64)
        v_scales = keep.tile([P, N], U8, name="v_scales", align_bytes=64)
        ds_pl = [keep.tile([P, PACK, N], BF16, name=f"ds_pl{g}", align_bytes=64) for g in range(G)]
        ds_bf = [keep.tile([P, N, PACK], BF16, name=f"ds_bf{g}", align_bytes=64) for g in range(G)]
        ds_codes = [keep.tile([P, N], U32, name=f"ds_codes{g}", align_bytes=64) for g in range(G)]
        ds_scales = [keep.tile([P, N], U8, name=f"ds_scales{g}", align_bytes=64) for g in range(G)]
        qm_bf = [keep.tile([P, D, PACK], BF16, name=f"qm_bf{g}", align_bytes=64) for g in range(G)]
        qm_codes = [keep.tile([P, D], U32, name=f"qm_codes{g}", align_bytes=64) for g in range(G)]
        qm_scales = [keep.tile([P, D], U8, name=f"qm_scales{g}", align_bytes=64) for g in range(G)]
        res = [keep.tile([P, N], F32, name=f"res{h}") for h in range(H)]

        dp = [[psum.tile([P, N], F32, name=f"dp{g}_{t}", tag=f"bank{g * PACK + t}") for t in range(PACK)] for g in range(G)]

        def quant(codes, scales, src):
            nc.vector.quantize_mx(out=codes.bitcast(FP8X4), scales=scales, in_=src.rearrange("p w j -> p (w j)"))

        def interleave_do(copy, g, m0, m1):
            copy(
                out=do_bf[g][:].rearrange("p (t m) j -> p m j t", t=PACK)[:, m0:m1],
                in_=do_raw[g][:].rearrange("p j (m t) -> p m j t", t=PACK)[:, m0:m1],
            )

        interleave_do(nc.scalar.copy, 0, 0, P)
        for t in range(PACK):
            nc.vector.tensor_copy(v_bf[:, :, t], v_raw[t][:].indirect(offsets[:]))
        quant(do_codes[0][:], do_scales[0][:], do_bf[0][:])
        quant(v_codes[:], v_scales[:], v_bf[:])
        interleave_do(nc.vector.tensor_copy, 1, 0, P // 2)
        interleave_do(nc.scalar.copy, 1, P // 2, P)
        quant(do_codes[1][:], do_scales[1][:], do_bf[1][:])

        def product_dp(g, t):
            bank = dp[g][t]
            cols = slice(t * P, (t + 1) * P)
            nc.tensor.matmul_mx(
                out=bank[:],
                lhsT=do_codes[g][:, cols].bitcast(FP8X4), lhsT_scale=do_scales[g][:, cols],
                rhs=v_codes[:].bitcast(FP8X4), rhs_scale=v_scales[:],
                start=True, stop=True,
            )
            return bank

        def p_plane(g, t):
            for i, (t0, w) in enumerate(P_CUTS):
                if t0 <= t < t0 + w:
                    return p_raw[g][i][:, t - t0, :]

        def weigh(g, t):
            bank = product_dp(g, t)
            if t == g:
                nc.scalar.activation(x[g][:], bank[:], IDENTITY, bias=ndlt[:, g, t:t + 1], scale=1.0)
                nc.gpsimd.tensor_tensor(ds_pl[g][:, t, :], x[g][:], p_plane(g, t), MULT)
                return
            nc.vector.scalar_tensor_tensor(ds_pl[g][:, t, :], bank[:], dlt[:, g, t:t + 1], p_plane(g, t), SUB, MULT)

        def interleave_ds(copy, g, t0, t1, cols):
            copy(
                out=ds_bf[g][:, cols, t0:t1].rearrange("p (c i) t -> p c t i", i=8),
                in_=ds_pl[g][:, t0:t1, cols].rearrange("p t (c i) -> p c t i", i=8),
            )

        def interleave_qm(copy, g, cols):
            copy(
                out=qm_bf[g][:, cols, :].rearrange("p (c i) t -> p c t i", i=4),
                in_=qm_raw[g][:, :, cols].rearrange("p t (c i) -> p c t i", i=4),
            )

        def quant_qm(g, cols):
            quant(qm_codes[g][:, cols], qm_scales[g][:, cols], qm_bf[g][:, cols, :])

        def quant_ds(g, cols):
            quant(ds_codes[g][:, cols], ds_scales[g][:, cols], ds_bf[g][:, cols, :])

        def product_dk(bank, h, n, g):
            d = slice(h * P, (h + 1) * P)
            nc.tensor.matmul_mx(
                out=bank[:],
                lhsT=qm_codes[g][:, d].bitcast(FP8X4), lhsT_scale=qm_scales[g][:, d],
                rhs=ds_codes[g][:, n].bitcast(FP8X4), rhs_scale=ds_scales[g][:, n],
                start=(g == 0), stop=(g == G - 1),
            )

        every = slice(0, N)
        slots = [slice(s * NH, (s + 1) * NH) for s in range(2)]

        nc.gpsimd.tensor_scalar(ndlt[:], dlt[:], -1.0, 0.0, MULT, ADD)
        for t in range(PACK):
            weigh(0, t)
        interleave_ds(nc.scalar.copy, 0, 0, 4, every)
        for t in range(PACK):
            weigh(1, t)
        interleave_qm(nc.vector.tensor_copy, 0, slice(0, D))
        quant_qm(0, slice(0, D))
        for s in range(2):
            interleave_ds(nc.scalar.copy, 1, 0, 4, slots[s])
        interleave_qm(nc.vector.tensor_copy, 1, slice(0, D))
        quant_ds(0, every)
        quant_ds(1, slots[0])
        quant_qm(1, slice(0, D))
        quant_ds(1, slots[1])
        dk = [[psum.tile([P, NH], F32, name=f"dk0_{s}", tag=f"bank{s}") for s in range(2)],
              [psum.tile([P, N], F32, name="dk1", tag="bank2")]]
        cuts = [slots, [every]]
        for h in range(H):
            for bank, n in zip(dk[h], cuts[h]):
                for g in range(G):
                    product_dk(bank, h, n, g)
                nc.scalar.copy(out=res[h][:, n], in_=bank[:])
        for h in range(H):
            for n in cuts[h]:
                nc.vector.tensor_copy(window[h][:].indirect(offsets[:, n.start // 16:n.stop // 16]), res[h][:, n])
            for k in range(2):
                span = slice(k * T // 2, (k + 1) * T // 2)
                (nc.sync if k == 0 else nc.scalar).dma_start(out[h * P:(h + 1) * P, span], window[h][:, span])
